import numpy as np
import ml_dtypes


def mxq(x, axis, fmt="e4m3"):
    dtype, down = {"e4m3": (ml_dtypes.float8_e4m3fn, 7), "e5m2": (ml_dtypes.float8_e5m2, 14)}[fmt]
    v = np.moveaxis(np.asarray(x, np.float32).astype(ml_dtypes.bfloat16).astype(np.float64), axis, -1)
    blocks = v.reshape(v.shape[:-1] + (-1, 32))
    amax = np.abs(blocks).max(-1, keepdims=True)
    byte = np.maximum(np.where(amax > 0, np.frexp(amax)[1] - 1 + 127, 0) - down, 1)
    scale = np.exp2(byte - 127.0)
    codes = (blocks / scale).astype(np.float32).astype(dtype).astype(np.float64)
    return np.moveaxis((codes * scale).reshape(v.shape), -1, axis)


WIDE = False


def mx_kscale(k):
    if not WIDE:
        return np.ones(k)
    levels = np.array([10, -10, 5, -5, 0])
    if k % 512:
        return np.exp2(np.random.permutation(np.resize(levels, k // 32))).repeat(32)
    a = np.empty((k // 512, 16))
    for p in range(k // 512):
        a[p, :8] = np.random.permutation(np.resize(levels, 8))
        for g in range(8):
            far = levels[np.abs(levels - a[p, g]) >= 10]
            a[p, g + 8] = far[np.random.randint(len(far))]
    return np.exp2(a.ravel()).repeat(32)


def f64(x):
    return np.asarray(x).astype(np.float64)


def striped(idx):
    return np.tile(idx.reshape(-1, 16).T, (8, 1)).astype(np.uint16)


def unstriped(offs):
    return offs[:16].T.reshape(-1).astype(np.int64)


E2M1 = np.array([0.0, 0.5, 1.0, 1.5, 2.0, 3.0, 4.0, 6.0, -0.0, -0.5, -1.0, -1.5, -2.0, -3.0, -4.0, -6.0])


def pack_weight(w, fmt):
    k, n = w.shape
    w = f64(np.asarray(w, np.float32).astype(ml_dtypes.bfloat16)).reshape(k // 32, 32, n)
    amax = np.abs(w).max(1)
    if fmt == "e4m3":
        byte = np.frexp(amax)[1] - 1 + 127 - 7
    else:
        mant, ex = np.frexp(amax / 6.0)
        byte = np.where(mant > 0.5, ex, ex - 1) + 127
    byte = np.clip(np.where(amax > 0, byte, 1), 1, 254)
    scaled = (w * np.exp2(127.0 - byte)[:, None, :]).reshape(k, n).astype(np.float32)
    by_word = np.ascontiguousarray(scaled.reshape(k // 512, 128, 4, n).transpose(0, 1, 3, 2))
    if fmt == "e4m3":
        words = by_word.astype(ml_dtypes.float8_e4m3fn).view(np.uint8)
    else:
        c = by_word.astype(ml_dtypes.float4_e2m1fn).view(np.uint8) & 0xF
        words = (c[..., 0::2] | (c[..., 1::2] << 4)).reshape(k // 512, 128, 2 * n)
    return np.ascontiguousarray(words), np.ascontiguousarray(byte.astype(np.uint8).reshape(k // 512, 16, n))


def unpack_weight(words, scales, fmt):
    g, _, n = scales.shape
    words = np.ascontiguousarray(words).reshape(g, 128, n, -1)
    if fmt == "e4m3":
        vals = words.view(ml_dtypes.float8_e4m3fn).astype(np.float64)
    else:
        nib = np.empty((g, 128, n, 4), np.uint8)
        nib[..., 0::2] = words & 0xF
        nib[..., 1::2] = words >> 4
        vals = E2M1[nib]
    vals = vals * np.repeat(np.exp2(scales.astype(np.float64) - 127.0), 8, axis=1)[..., None]
    return vals.transpose(0, 1, 3, 2).reshape(g * 512, n)


def gelu(v):
    return 0.5 * v * (1.0 + np.tanh(np.sqrt(2.0 / np.pi) * (v + 0.044715 * v**3)))


def striped8(idx):
    return np.concatenate([v.reshape(-1, 16).T for v in idx]).astype(np.uint16)


def unstriped8(offs):
    return np.stack([offs[16 * g:16 * g + 16].T.reshape(-1) for g in range(8)]).astype(np.int64)


def heads(h, wgt, idx8):
    r = np.arange(h.shape[0])
    return wgt[r // 4 % 128] * h[r[:, None], idx8[r % 512 // 64]]


def put_heads(h, wgs, idx8, t2):
    r = np.arange(h.shape[0])
    page = np.zeros((h.shape[0], t2))
    page[r[:, None], idx8[r % 512 // 64]] = wgs[r // 4 % 128] * h
    return page


K, T, S, T2, P, H, N = 1024, 2048, 1024, 2048, 1024, 512, 384

def setup_inputs():
    n = np.random.standard_normal
    s = mx_kscale(K)[:, None]
    u = mx_kscale(H)[:, None]
    d = {}
    d["tab_words"], d["tab_scales"] = pack_weight(n((K, T)) * s, "e4m3")
    d["offs"] = striped(np.random.permutation(T)[:S])
    d["w1"] = (n((K, H)) / K**0.5 / s * u.T).astype(np.float32)
    d["w2_words"], d["w2_scales"] = pack_weight(1.4 * n((K, H)) / K**0.5 / s * u.T, "e2m1")
    d["w3"] = (1.2 * n((K, H)) / K**0.5 / s * u.T).astype(np.float32)
    d["wgs"] = np.repeat(np.random.uniform(0.5, 2.0, (8, S)), 16, axis=0).astype(np.float32)
    d["offs2"] = striped8(np.stack([np.random.permutation(T2)[:S] for _ in range(8)]))
    d["wgt"] = np.repeat(np.random.uniform(0.5, 2.0, (8, P)), 16, axis=0).astype(np.float32)
    d["offs3"] = striped8(np.stack([np.random.permutation(T2)[:P] for _ in range(8)]))
    d["surf"] = (1.2 * n((H, P)) * u).astype(np.float32)
    d["w4_words"], d["w4_scales"] = pack_weight(0.9 * n((H, N)) / H**0.5 / u, "e4m3")
    return d

def reference(tab_words, tab_scales, offs, w1, w2_words, w2_scales, w3, wgs, offs2, wgt, offs3, surf, w4_words, w4_scales):
    v = unpack_weight(tab_words, tab_scales, "e4m3")[:, unstriped(offs)]
    base = mxq(f64(w1), 0, "e4m3").T @ v
    more = unpack_weight(w2_words, w2_scales, "e2m1").T @ v
    less = mxq(f64(w3), 0, "e4m3").T @ v
    h = base + np.abs(more) - np.abs(less)
    page = put_heads(h, f64(wgs), unstriped8(offs2), T2)
    x = heads(page, f64(wgt), unstriped8(offs3))
    z = np.maximum(x, f64(surf))
    y = unpack_weight(w4_words, w4_scales, "e4m3").T @ mxq(z, 0, "e4m3")
    return np.tanh(y)

@@ -1,0 +1,257 @@
+from contextlib import ExitStack
+
+import concourse.mybir as mybir
+from concourse.masks import make_identity
+
+K, T, S, T2, PM, H, N = 1024, 2048, 1024, 2048, 1024, 512, 384
+FLOPS = 3623878656
+
+F32 = mybir.dt.float32
+BF16 = mybir.dt.bfloat16
+I32 = mybir.dt.int32
+U32 = mybir.dt.uint32
+U16 = mybir.dt.uint16
+U8 = mybir.dt.uint8
+FP8X4 = mybir.dt.float8_e4m3fn_x4
+FP4X4 = mybir.dt.float4_e2m1fn_x4
+ACT = mybir.ActivationFunctionType
+ALU = mybir.AluOpType
+
+P = 128
+SCATTER_CHUNKS = (128, 128, 256, 256, 256)
+GATHER_CHUNKS = (256, 256, 256, 128, 128)
+
+
+def tile_list_obstacle_fault_scores_kernel(
+    tc, tab_words, tab_scales, offs, w1, w2_words, w2_scales, w3, wgs, offs2, wgt, offs3, surf, w4_words, w4_scales, out
+):
+    nc = tc.nc
+    with ExitStack() as ctx:
+        keep = ctx.enter_context(tc.tile_pool(name="keep", bufs=1))
+        ring = ctx.enter_context(tc.tile_pool(name="ring", bufs=2))
+        shared = ctx.enter_context(tc.tile_pool(name="shared", bufs=1))
+        psum = ctx.enter_context(tc.psum_pool(name="psum", bufs=2))
+
+        list1 = keep.tile([P, S // 16], U16, name="list1")
+        list2 = keep.tile([P, S // 16], U16, name="list2")
+        list3 = keep.tile([P, PM // 16], U16, name="list3")
+        tab = [keep.tile([P, T], I32, name="tab%d" % a, align_bytes=64) for a in range(2)]
+        tab_sc = keep.tile([P, 2 * T], U8, name="tab_sc", align_bytes=64)
+        v = {}
+        v_sc = {}
+        w2c = keep.tile([P, 2 * 2 * H], U8, name="w2c", align_bytes=64)
+        w2s = keep.tile([P, 2 * H], U8, name="w2s", align_bytes=64)
+        w4c = keep.tile([P, N], I32, name="w4c", align_bytes=64)
+        w4s = keep.tile([P, N], U8, name="w4s", align_bytes=64)
+        w3_raw = [keep.tile([P, 4, H], F32, name="w3_raw%d" % a) for a in range(2)]
+        w1_raw0 = keep.tile([P, 4, H], F32, name="w1_raw0")
+        w1_raw1 = [keep.tile([P, 4, H // 2], F32, name="w1_raw1%d" % u) for u in range(2)]
+        wq = {}
+        for nm in ("w1", "w3"):
+            for a in range(2):
+                wq[nm, a] = (
+                    None if (nm, a) == ("w1", 1) else keep.tile([P, H, 4], BF16, name="%sb%d" % (nm, a), align_bytes=64),
+                    keep.tile([P, H], U32, name="%sc%d" % (nm, a), align_bytes=64),
+                    keep.tile([P, H], U8, name="%ss%d" % (nm, a), align_bytes=64),
+                )
+        pages = [keep.tile([P, T2], F32, name="page%d" % t) for t in range(4)]
+        ident = keep.tile([P, P], F32, name="ident")
+
+        nc.gpsimd.memset(tab_sc[:, 0:T].bitcast(I32), 0)
+        nc.vector.memset(tab_sc[:, T : 2 * T].bitcast(I32), 0)
+        nc.gpsimd.memset(w2s[:].bitcast(I32), 0)
+        nc.gpsimd.memset(w4s[:].bitcast(I32), 0)
+        make_identity(nc, ident[:])
+
+        def load_words(a):
+            nc.sync.dma_start(out=tab[a][:], in_=tab_words[a].rearrange("p t i -> p (t i)").bitcast(I32))
+
+        nc.sync.dma_start(list1[:], offs)
+        nc.sync.dma_start(list2[:], offs2)
+        nc.sync.dma_start(list3[:], offs3)
+        nc.sync.dma_start(out=w3_raw[0][:], in_=w3[0:512, :].rearrange("(p j) c -> p j c", j=4))
+        for q in range(4):
+            nc.sync.dma_start(
+                out=tab_sc[32 * q : 32 * q + 4, :].bitcast(I32).rearrange("r (a c) -> r a c", a=2),
+                in_=tab_scales.bitcast(I32)[:, 4 * q : 4 * q + 4, :].rearrange("a r c -> r a c"),
+            )
+        load_words(0)
+        nc.sync.dma_start(out=w3_raw[1][:], in_=w3[512:1024, :].rearrange("(p j) c -> p j c", j=4))
+        load_words(1)
+        nc.sync.dma_start(
+            out=w2c[:].bitcast(I32).rearrange("p (a c) -> p a c", a=2), in_=w2_words.bitcast(I32).rearrange("a p c -> p a c")
+        )
+        for q in range(4):
+            nc.sync.dma_start(
+                out=w2s[32 * q : 32 * q + 4, :].bitcast(I32).rearrange("r (a c) -> r a c", a=2),
+                in_=w2_scales.bitcast(I32)[:, 4 * q : 4 * q + 4, :].rearrange("a r c -> r a c"),
+            )
+        nc.sync.dma_start(out=w1_raw0[:], in_=w1[0:512, :].rearrange("(p j) c -> p j c", j=4))
+        for u in range(2):
+            nc.sync.dma_start(
+                out=w1_raw1[u][:], in_=w1[512:1024, :].rearrange("(p j) c -> p j c", j=4)[:, :, 256 * u : 256 * (u + 1)]
+            )
+        nc.sync.dma_start(out=w4c[:], in_=w4_words[0].rearrange("p c i -> p (c i)").bitcast(I32))
+        for q in range(4):
+            nc.sync.dma_start(out=w4s[32 * q : 32 * q + 4, :].bitcast(I32), in_=w4_scales.bitcast(I32)[0, 4 * q : 4 * q + 4, :])
+
+        def gather_words(a, j0, n):
+            if (a, j0) == (1, 512):
+                v[a, j0] = shared.tile([P, n], U32, name="v_late", align_bytes=64, offset=0)
+            else:
+                v[a, j0] = keep.tile([P, n], U32, name="v%d_%d" % (a, j0), align_bytes=64)
+            nc.vector.tensor_copy(v[a, j0][:], tab[a][:].bitcast(U32).indirect(list1[:, j0 // 16 : (j0 + n) // 16]))
+
+        def walk_out(dst):
+            return dst.rearrange("p (c i) t -> p c t i", i=4)
+
+        def walk_in(src):
+            return src.rearrange("p t (c i) -> p c t i", i=4)
+
+        def quantize(key):
+            grouped, codes, scales = wq[key]
+            nc.vector.quantize_mx(out=codes[:].bitcast(FP8X4), scales=scales[:], in_=grouped[:].rearrange("p c t -> p (c t)"))
+
+        def gather_scales(a, j0, n):
+            if (a, j0) == (1, 512):
+                v_sc[a, j0] = shared.tile([P, n], U8, name="v_sc_late", align_bytes=64, offset=2048)
+            else:
+                v_sc[a, j0] = keep.tile([P, n], U8, name="v_sc%d_%d" % (a, j0), align_bytes=64)
+            nc.vector.tensor_copy(
+                v_sc[a, j0][:], tab_sc[:, T * a : T * (a + 1)].indirect(list1[:, j0 // 16 : (j0 + n) // 16])
+            )
+
+        for a in range(2):
+            gather_scales(a, 0, 512)
+        for a in range(2):
+            gather_words(a, 0, 512)
+        for a in range(2):
+            nc.scalar.copy(walk_out(wq["w3", a][0][:]), walk_in(w3_raw[a][:]))
+            quantize(("w3", a))
+        nc.vector.tensor_copy(walk_out(wq["w1", 0][0][:]), walk_in(w1_raw0[:]))
+        quantize(("w1", 0))
+        for u in range(2):
+            if u == 0:
+                grouped = keep.tile([P, H // 2, 4], BF16, name="w1_first", align_bytes=64)
+            else:
+                grouped = shared.tile([P, H // 2, 4], BF16, name="w1_last", align_bytes=64, offset=512)
+            nc.vector.tensor_copy(walk_out(grouped[:]), walk_in(w1_raw1[u][:]))
+            cols = slice(256 * u, 256 * (u + 1))
+            nc.vector.quantize_mx(
+                out=wq["w1", 1][1][:, cols].bitcast(FP8X4), scales=wq["w1", 1][2][:, cols], in_=grouped[:].rearrange("p c t -> p (c t)")
+            )
+        wgs_sb = keep.tile([P, S], F32, name="wgs_sb", tag="w3_raw0")
+        wgt_sb = keep.tile([P, PM], F32, name="wgt_sb", tag="w1_raw10")
+        surf_sb = [keep.tile([P, 4, PM // 2], F32, name="surf_sb", tag=tag) for tag in ("w3_raw1", "w1_raw0")]
+        nc.sync.dma_start(out=wgs_sb[:], in_=wgs)
+        nc.sync.dma_start(out=wgt_sb[:], in_=wgt)
+        for u in range(2):
+            nc.sync.dma_start(out=surf_sb[u][:], in_=surf.rearrange("(p t) m -> p t m", t=4)[:, :, 512 * u : 512 * (u + 1)])
+        for t in range(4):
+            nc.gpsimd.memset(pages[t][:], 0.0)
+        for a in range(2):
+            gather_words(a, 512, 512)
+            gather_scales(a, 512, 512)
+
+        def product(tag, j0, fp4):
+            bank = psum.tile([P, H], F32, name=tag, tag=tag)
+            for a in range(2):
+                if fp4:
+                    rhs = w2c[:, 2 * H * a : 2 * H * (a + 1)].bitcast(FP4X4)
+                    rhs_sc = w2s[:, H * a : H * (a + 1)]
+                else:
+                    rhs = wq[tag, a][1][:].bitcast(FP8X4)
+                    rhs_sc = wq[tag, a][2][:]
+                nc.tensor.matmul_mx(
+                    out=bank[:], lhsT=v[a, j0 // 512 * 512][:, j0 % 512 : j0 % 512 + P].bitcast(FP8X4), lhsT_scale=v_sc[a, j0 // 512 * 512][:, j0 % 512 : j0 % 512 + P],
+                    rhs=rhs, rhs_scale=rhs_sc, start=(a == 0), stop=(a == 1),
+                )
+            return bank[:].rearrange("j (m t) -> j t m", t=4)
+
+        def token_tile(j0, h_out):
+            more = ring.tile([P, 4, P], F32, name="more", tag="more", bufs=2)
+            less = ring.tile([P, 4, P], F32, name="less", tag="less", bufs=2)
+            neg = ring.tile([P, 4, P], F32, name="neg", tag="neg", bufs=2)
+            base = ring.tile([P, 4, P], F32, name="base", tag="base", bufs=2)
+            nc.scalar.activation(more[:], product("w2", j0, True), ACT.Abs)
+            nc.scalar.activation(less[:], product("w3", j0, False), ACT.Abs)
+            nc.scalar.activation(neg[:], less[:], ACT.Copy, scale=-1.0)
+            nc.scalar.copy(base[:], product("w1", j0, False))
+            acc = psum.tile([P, 4, P], F32, name="acc", tag="acc")
+            for e, term in enumerate((more, neg, base)):
+                for t in range(4):
+                    nc.tensor.matmul(
+                        acc[:, t, :], term[:, t, :], ident[:], is_transpose=True, start=(e == 0 and t == 0), stop=(e == 2 and t == 3)
+                    )
+            nc.scalar.copy(h_out, acc[:])
+
+        j0 = 0
+        for ci, n in enumerate(SCATTER_CHUNKS):
+            h = keep.tile([P, 4, n], F32, name="h%d" % ci)
+            for u in range(n // P):
+                token_tile(j0 + P * u, h[:, :, P * u : P * (u + 1)])
+            for t in range(4):
+                nc.vector.tensor_tensor(
+                    pages[t][:].indirect(list2[:, j0 // 16 : (j0 + n) // 16]), h[:, t, :], wgs_sb[:, j0 : j0 + n], ALU.mult
+                )
+            j0 += n
+
+        starts = [sum(GATHER_CHUNKS[:c]) for c in range(len(GATHER_CHUNKS))]
+        last = len(GATHER_CHUNKS) - 1
+        xs, zs, zq = {}, {}, {}
+
+        def gather(c):
+            m0, n = starts[c], GATHER_CHUNKS[c]
+            x = keep.tile([P, 4, n], F32, name="x", tag="x")
+            for t in range(4):
+                nc.vector.tensor_tensor(
+                    x[:, t, :], pages[t][:].indirect(list3[:, m0 // 16 : (m0 + n) // 16]), wgt_sb[:, m0 : m0 + n], ALU.mult
+                )
+            xs[c] = x
+
+        def maximum(c):
+            m0, n = starts[c], GATHER_CHUNKS[c]
+            s = surf_sb[m0 // 512][:, :, m0 % 512 : m0 % 512 + n]
+            z = keep.tile([P, n, 4], BF16, name="z%d" % c, align_bytes=64)
+            if c == last:
+                nc.vector.tensor_tensor(walk_out(z[:]), walk_in(xs[c][:]), walk_in(s), ALU.max)
+            else:
+                planes = keep.tile([P, 4, n], BF16, name="planes", tag="planes", align_bytes=64)
+                nc.vector.tensor_tensor(planes[:], xs[c][:], s, ALU.max)
+                nc.scalar.copy(walk_out(z[:]), walk_in(planes[:]))
+            zs[c] = z
+
+        def quantize_z(c):
+            n = GATHER_CHUNKS[c]
+            zc = keep.tile([P, n], U32, name="zc%d" % c, align_bytes=64)
+            zsc = keep.tile([P, n], U8, name="zsc%d" % c, align_bytes=64)
+            nc.vector.quantize_mx(out=zc[:].bitcast(FP8X4), scales=zsc[:], in_=zs[c][:].rearrange("p m t -> p (m t)"))
+            zq[c] = (zc, zsc)
+
+        def finish(c):
+            m0, n = starts[c], GATHER_CHUNKS[c]
+            zc, zsc = zq[c]
+            res = keep.tile([P, 3, n], F32, name="res%d" % c)
+            per_bank = min(3, 512 // n)
+            for b0 in range(0, 3, per_bank):
+                nb = min(per_bank, 3 - b0)
+                tag = ("w1", "w2", "w3")[(b0 + c) % 3]
+                bank = psum.tile([P, nb, n], F32, name=tag, tag=tag)
+                for b in range(nb):
+                    cols = slice(P * (b0 + b), P * (b0 + b + 1))
+                    nc.tensor.matmul_mx(
+                        out=bank[:, b, :], lhsT=w4c[:, cols].bitcast(FP8X4), lhsT_scale=w4s[:, cols],
+                        rhs=zc[:].bitcast(FP8X4), rhs_scale=zsc[:], start=True, stop=True,
+                    )
+                nc.scalar.activation(res[:, b0 : b0 + nb, :], bank[:], ACT.Tanh)
+            nc.sync.dma_start(out=out.rearrange("(b p) m -> p b m", p=P)[:, :, m0 : m0 + n], in_=res[:])
+
+        for c in range(last + 1):
+            gather(c)
+            if c >= 1:
+                quantize_z(c - 1)
+            maximum(c)
+            if c >= 1:
+                finish(c - 1)
+        quantize_z(last)
+        finish(last)

@@ -18,7 +18,8 @@ ACT = mybir.ActivationFunctionType
 ALU = mybir.AluOpType
 
 P = 128
-SCATTER_CHUNKS = (128, 128, 256, 256, 256)
+BANKS = {"w1": 2, "w2": 1, "w3": 1}
+SCATTER_CHUNKS = (128, 128, 128, 128, 128, 128, 256)
 GATHER_CHUNKS = (256, 256, 256, 128, 128)
 
 
@@ -69,15 +70,13 @@ def tile_list_obstacle_fault_scores_kernel(
         nc.sync.dma_start(list1[:], offs)
         nc.sync.dma_start(list2[:], offs2)
         nc.sync.dma_start(list3[:], offs3)
-        nc.sync.dma_start(out=w3_raw[0][:], in_=w3[0:512, :].rearrange("(p j) c -> p j c", j=4))
+        load_words(0)
         for q in range(4):
-            nc.sync.dma_start(
+            nc.scalar.dma_start(
                 out=tab_sc[32 * q : 32 * q + 4, :].bitcast(I32).rearrange("r (a c) -> r a c", a=2),
                 in_=tab_scales.bitcast(I32)[:, 4 * q : 4 * q + 4, :].rearrange("a r c -> r a c"),
             )
-        load_words(0)
-        nc.sync.dma_start(out=w3_raw[1][:], in_=w3[512:1024, :].rearrange("(p j) c -> p j c", j=4))
-        load_words(1)
+        nc.sync.dma_start(out=w3_raw[0][:], in_=w3[0:512, :].rearrange("(p j) c -> p j c", j=4))
         nc.sync.dma_start(
             out=w2c[:].bitcast(I32).rearrange("p (a c) -> p a c", a=2), in_=w2_words.bitcast(I32).rearrange("a p c -> p a c")
         )
@@ -86,6 +85,8 @@ def tile_list_obstacle_fault_scores_kernel(
                 out=w2s[32 * q : 32 * q + 4, :].bitcast(I32).rearrange("r (a c) -> r a c", a=2),
                 in_=w2_scales.bitcast(I32)[:, 4 * q : 4 * q + 4, :].rearrange("a r c -> r a c"),
             )
+        nc.sync.dma_start(out=w3_raw[1][:], in_=w3[512:1024, :].rearrange("(p j) c -> p j c", j=4))
+        load_words(1)
         nc.sync.dma_start(out=w1_raw0[:], in_=w1[0:512, :].rearrange("(p j) c -> p j c", j=4))
         for u in range(2):
             nc.sync.dma_start(
@@ -154,7 +155,7 @@ def tile_list_obstacle_fault_scores_kernel(
             gather_scales(a, 512, 512)
 
         def product(tag, j0, fp4):
-            bank = psum.tile([P, H], F32, name=tag, tag=tag)
+            bank = psum.tile([P, H], F32, name=tag, tag=tag, bufs=BANKS[tag])
             for a in range(2):
                 if fp4:
                     rhs = w2c[:, 2 * H * a : 2 * H * (a + 1)].bitcast(FP4X4)
@@ -235,8 +236,7 @@ def tile_list_obstacle_fault_scores_kernel(
             per_bank = min(3, 512 // n)
             for b0 in range(0, 3, per_bank):
                 nb = min(per_bank, 3 - b0)
-                tag = ("w1", "w2", "w3")[(b0 + c) % 3]
-                bank = psum.tile([P, nb, n], F32, name=tag, tag=tag)
+                bank = psum.tile([P, nb, n], F32, name="y", tag="y", bufs=2)
                 for b in range(nb):
                     cols = slice(P * (b0 + b), P * (b0 + b + 1))
                     nc.tensor.matmul_mx(

@@ -18,7 +18,6 @@ ACT = mybir.ActivationFunctionType
 ALU = mybir.AluOpType
 
 P = 128
-BANKS = {"w1": 2, "w2": 1, "w3": 1}
 SCATTER_CHUNKS = (128, 128, 128, 128, 128, 128, 256)
 GATHER_CHUNKS = (256, 256, 256, 128, 128)
 
@@ -31,7 +30,7 @@ def tile_list_obstacle_fault_scores_kernel(
         keep = ctx.enter_context(tc.tile_pool(name="keep", bufs=1))
         ring = ctx.enter_context(tc.tile_pool(name="ring", bufs=2))
         shared = ctx.enter_context(tc.tile_pool(name="shared", bufs=1))
-        psum = ctx.enter_context(tc.psum_pool(name="psum", bufs=2))
+        psum = ctx.enter_context(tc.psum_pool(name="psum", bufs=1))
 
         list1 = keep.tile([P, S // 16], U16, name="list1")
         list2 = keep.tile([P, S // 16], U16, name="list2")
@@ -77,9 +76,6 @@ def tile_list_obstacle_fault_scores_kernel(
                 in_=tab_scales.bitcast(I32)[:, 4 * q : 4 * q + 4, :].rearrange("a r c -> r a c"),
             )
         nc.sync.dma_start(out=w3_raw[0][:], in_=w3[0:512, :].rearrange("(p j) c -> p j c", j=4))
-        nc.sync.dma_start(
-            out=w2c[:].bitcast(I32).rearrange("p (a c) -> p a c", a=2), in_=w2_words.bitcast(I32).rearrange("a p c -> p a c")
-        )
         for q in range(4):
             nc.sync.dma_start(
                 out=w2s[32 * q : 32 * q + 4, :].bitcast(I32).rearrange("r (a c) -> r a c", a=2),
@@ -92,6 +88,9 @@ def tile_list_obstacle_fault_scores_kernel(
             nc.sync.dma_start(
                 out=w1_raw1[u][:], in_=w1[512:1024, :].rearrange("(p j) c -> p j c", j=4)[:, :, 256 * u : 256 * (u + 1)]
             )
+        nc.sync.dma_start(
+            out=w2c[:].bitcast(I32).rearrange("p (a c) -> p a c", a=2), in_=w2_words.bitcast(I32).rearrange("a p c -> p a c")
+        )
         nc.sync.dma_start(out=w4c[:], in_=w4_words[0].rearrange("p c i -> p (c i)").bitcast(I32))
         for q in range(4):
             nc.sync.dma_start(out=w4s[32 * q : 32 * q + 4, :].bitcast(I32), in_=w4_scales.bitcast(I32)[0, 4 * q : 4 * q + 4, :])
@@ -114,8 +113,8 @@ def tile_list_obstacle_fault_scores_kernel(
             nc.vector.quantize_mx(out=codes[:].bitcast(FP8X4), scales=scales[:], in_=grouped[:].rearrange("p c t -> p (c t)"))
 
         def gather_scales(a, j0, n):
-            if (a, j0) == (1, 512):
-                v_sc[a, j0] = shared.tile([P, n], U8, name="v_sc_late", align_bytes=64, offset=2048)
+            if j0 == 512:
+                v_sc[a, j0] = shared.tile([P, n], U8, name="v_sc_late%d" % a, align_bytes=64, offset=2048 + 512 * a)
             else:
                 v_sc[a, j0] = keep.tile([P, n], U8, name="v_sc%d_%d" % (a, j0), align_bytes=64)
             nc.vector.tensor_copy(
@@ -135,7 +134,7 @@ def tile_list_obstacle_fault_scores_kernel(
             if u == 0:
                 grouped = keep.tile([P, H // 2, 4], BF16, name="w1_first", align_bytes=64)
             else:
-                grouped = shared.tile([P, H // 2, 4], BF16, name="w1_last", align_bytes=64, offset=512)
+                grouped = shared.tile([P, H // 2, 4], BF16, name="w1_last", align_bytes=64, offset=1024)
             nc.vector.tensor_copy(walk_out(grouped[:]), walk_in(w1_raw1[u][:]))
             cols = slice(256 * u, 256 * (u + 1))
             nc.vector.quantize_mx(
@@ -149,13 +148,17 @@ def tile_list_obstacle_fault_scores_kernel(
         for u in range(2):
             nc.sync.dma_start(out=surf_sb[u][:], in_=surf.rearrange("(p t) m -> p t m", t=4)[:, :, 512 * u : 512 * (u + 1)])
         for t in range(4):
-            nc.gpsimd.memset(pages[t][:], 0.0)
+            nc.vector.memset(pages[t][:], 0.0)
         for a in range(2):
             gather_words(a, 512, 512)
             gather_scales(a, 512, 512)
 
+        def bank_tag(role, j0):
+            i = j0 // P
+            return "bank%d" % (4 * (i % 2) + (role + 2 * (i // 2)) % 4)
+
         def product(tag, j0, fp4):
-            bank = psum.tile([P, H], F32, name=tag, tag=tag, bufs=BANKS[tag])
+            bank = psum.tile([P, H], F32, name=tag, tag=bank_tag({"w2": 0, "w3": 1, "w1": 2}[tag], j0))
             for a in range(2):
                 if fp4:
                     rhs = w2c[:, 2 * H * a : 2 * H * (a + 1)].bitcast(FP4X4)
@@ -178,8 +181,8 @@ def tile_list_obstacle_fault_scores_kernel(
             nc.scalar.activation(less[:], product("w3", j0, False), ACT.Abs)
             nc.scalar.activation(neg[:], less[:], ACT.Copy, scale=-1.0)
             nc.scalar.copy(base[:], product("w1", j0, False))
-            acc = psum.tile([P, 4, P], F32, name="acc", tag="acc")
-            for e, term in enumerate((more, neg, base)):
+            acc = psum.tile([P, 4, P], F32, name="acc", tag=bank_tag(3, j0))
+            for e, term in enumerate((neg, more, base) if j0 == 0 else (base, more, neg)):
                 for t in range(4):
                     nc.tensor.matmul(
                         acc[:, t, :], term[:, t, :], ident[:], is_transpose=True, start=(e == 0 and t == 0), stop=(e == 2 and t == 3)
@@ -236,7 +239,7 @@ def tile_list_obstacle_fault_scores_kernel(
             per_bank = min(3, 512 // n)
             for b0 in range(0, 3, per_bank):
                 nb = min(per_bank, 3 - b0)
-                bank = psum.tile([P, nb, n], F32, name="y", tag="y", bufs=2)
+                bank = psum.tile([P, nb, n], F32, name="y", tag="bank%d" % ((2 * c + b0 // per_bank) % 8))
                 for b in range(nb):
                     cols = slice(P * (b0 + b), P * (b0 + b + 1))
                     nc.tensor.matmul_mx(

@@ -18,7 +18,7 @@ ACT = mybir.ActivationFunctionType
 ALU = mybir.AluOpType
 
 P = 128
-SCATTER_CHUNKS = (128, 128, 128, 128, 128, 128, 256)
+SCATTER_CHUNKS = (128, 128, 128, 128, 256, 256)
 GATHER_CHUNKS = (256, 256, 256, 128, 128)
 
 
@@ -155,7 +155,7 @@ def tile_list_obstacle_fault_scores_kernel(
 
         def bank_tag(role, j0):
             i = j0 // P
-            return "bank%d" % (4 * (i % 2) + (role + 2 * (i // 2)) % 4)
+            return "bank%d" % (4 * (i % 2) + (role + 2 * min(i // 2, 1)) % 4)
 
         def product(tag, j0, fp4):
             bank = psum.tile([P, H], F32, name=tag, tag=bank_tag({"w2": 0, "w3": 1, "w1": 2}[tag], j0))
@@ -206,7 +206,7 @@ def tile_list_obstacle_fault_scores_kernel(
 
         def gather(c):
             m0, n = starts[c], GATHER_CHUNKS[c]
-            x = keep.tile([P, 4, n], F32, name="x", tag="x")
+            x = ring.tile([P, 4, n], F32, name="x", tag="x", bufs=2)
             for t in range(4):
                 nc.vector.tensor_tensor(
                     x[:, t, :], pages[t][:].indirect(list3[:, m0 // 16 : (m0 + n) // 16]), wgt_sb[:, m0 : m0 + n], ALU.mult

@@ -3,7 +3,7 @@ from contextlib import ExitStack
 import concourse.mybir as mybir
 from concourse.masks import make_identity
 
-K, T, S, T2, PM, H, N = 1024, 2048, 1024, 2048, 1024, 512, 384
+T, S, T2, PM, H, N = 2048, 1024, 2048, 1024, 512, 384
 FLOPS = 3623878656
 
 F32 = mybir.dt.float32
@@ -18,8 +18,27 @@ ACT = mybir.ActivationFunctionType
 ALU = mybir.AluOpType
 
 P = 128
-SCATTER_CHUNKS = (128, 128, 128, 128, 256, 256)
-GATHER_CHUNKS = (256, 256, 256, 128, 128)
+PACK = 4
+PASSES = 2
+K_PASS = P * PACK
+QUADRANTS = 4
+HALF = S // 2
+BANK = 512
+BLOCKS = N // P
+CHUNKS = (256, 256, 256, 128, 128)
+MORE, LESS, BASE, SUM = 0, 1, 2, 3
+
+
+def list_slice(offsets, first, count):
+    return offsets[:, first // 16 : (first + count) // 16]
+
+
+def walk_out(dst):
+    return dst.rearrange("p (c i) t -> p c t i", i=4)
+
+
+def walk_in(src):
+    return src.rearrange("p t (c i) -> p c t i", i=4)
 
 
 def tile_list_obstacle_fault_scores_kernel(
@@ -35,26 +54,23 @@ def tile_list_obstacle_fault_scores_kernel(
         list1 = keep.tile([P, S // 16], U16, name="list1")
         list2 = keep.tile([P, S // 16], U16, name="list2")
         list3 = keep.tile([P, PM // 16], U16, name="list3")
-        tab = [keep.tile([P, T], I32, name="tab%d" % a, align_bytes=64) for a in range(2)]
-        tab_sc = keep.tile([P, 2 * T], U8, name="tab_sc", align_bytes=64)
-        v = {}
-        v_sc = {}
-        w2c = keep.tile([P, 2 * 2 * H], U8, name="w2c", align_bytes=64)
-        w2s = keep.tile([P, 2 * H], U8, name="w2s", align_bytes=64)
+        tab = [keep.tile([P, T], I32, name="tab%d" % a, align_bytes=64) for a in range(PASSES)]
+        tab_sc = keep.tile([P, PASSES * T], U8, name="tab_sc", align_bytes=64)
+        w2c = keep.tile([P, PASSES * 2 * H], U8, name="w2c", align_bytes=64)
+        w2s = keep.tile([P, PASSES * H], U8, name="w2s", align_bytes=64)
         w4c = keep.tile([P, N], I32, name="w4c", align_bytes=64)
         w4s = keep.tile([P, N], U8, name="w4s", align_bytes=64)
-        w3_raw = [keep.tile([P, 4, H], F32, name="w3_raw%d" % a) for a in range(2)]
-        w1_raw0 = keep.tile([P, 4, H], F32, name="w1_raw0")
-        w1_raw1 = [keep.tile([P, 4, H // 2], F32, name="w1_raw1%d" % u) for u in range(2)]
-        wq = {}
-        for nm in ("w1", "w3"):
-            for a in range(2):
-                wq[nm, a] = (
-                    None if (nm, a) == ("w1", 1) else keep.tile([P, H, 4], BF16, name="%sb%d" % (nm, a), align_bytes=64),
-                    keep.tile([P, H], U32, name="%sc%d" % (nm, a), align_bytes=64),
-                    keep.tile([P, H], U8, name="%ss%d" % (nm, a), align_bytes=64),
-                )
-        pages = [keep.tile([P, T2], F32, name="page%d" % t) for t in range(4)]
+        w3_raw = [keep.tile([P, PACK, H], F32, name="w3_raw%d" % a) for a in range(PASSES)]
+        w1_raw0 = keep.tile([P, PACK, H], F32, name="w1_raw0")
+        w1_raw1 = [keep.tile([P, PACK, H // 2], F32, name="w1_raw1%d" % u) for u in range(2)]
+        rounded, codes, scales = {}, {}, {}
+        for name in ("w1", "w3"):
+            for a in range(PASSES):
+                if (name, a) != ("w1", 1):
+                    rounded[name, a] = keep.tile([P, H, PACK], BF16, name="%sb%d" % (name, a), align_bytes=64)
+                codes[name, a] = keep.tile([P, H], U32, name="%sc%d" % (name, a), align_bytes=64)
+                scales[name, a] = keep.tile([P, H], U8, name="%ss%d" % (name, a), align_bytes=64)
+        pages = [keep.tile([P, T2], F32, name="page%d" % t) for t in range(PACK)]
         ident = keep.tile([P, P], F32, name="ident")
 
         nc.gpsimd.memset(tab_sc[:, 0:T].bitcast(I32), 0)
@@ -63,194 +79,210 @@ def tile_list_obstacle_fault_scores_kernel(
         nc.gpsimd.memset(w4s[:].bitcast(I32), 0)
         make_identity(nc, ident[:])
 
-        def load_words(a):
+        def load_table_words(a):
             nc.sync.dma_start(out=tab[a][:], in_=tab_words[a].rearrange("p t i -> p (t i)").bitcast(I32))
+
+        def load_scale_rows(queue, tile, rows):
+            for q in range(QUADRANTS):
+                queue.dma_start(
+                    out=tile[32 * q : 32 * q + 4, :].bitcast(I32).rearrange("r (a c) -> r a c", a=PASSES),
+                    in_=rows.bitcast(I32)[:, 4 * q : 4 * q + 4, :].rearrange("a r c -> r a c"),
+                )
+
+        def weight_pass(w, a):
+            return w[K_PASS * a : K_PASS * (a + 1), :].rearrange("(p i) c -> p i c", i=PACK)
 
         nc.sync.dma_start(list1[:], offs)
         nc.sync.dma_start(list2[:], offs2)
         nc.sync.dma_start(list3[:], offs3)
-        load_words(0)
-        for q in range(4):
-            nc.scalar.dma_start(
-                out=tab_sc[32 * q : 32 * q + 4, :].bitcast(I32).rearrange("r (a c) -> r a c", a=2),
-                in_=tab_scales.bitcast(I32)[:, 4 * q : 4 * q + 4, :].rearrange("a r c -> r a c"),
-            )
-        nc.sync.dma_start(out=w3_raw[0][:], in_=w3[0:512, :].rearrange("(p j) c -> p j c", j=4))
-        for q in range(4):
-            nc.sync.dma_start(
-                out=w2s[32 * q : 32 * q + 4, :].bitcast(I32).rearrange("r (a c) -> r a c", a=2),
-                in_=w2_scales.bitcast(I32)[:, 4 * q : 4 * q + 4, :].rearrange("a r c -> r a c"),
-            )
-        nc.sync.dma_start(out=w3_raw[1][:], in_=w3[512:1024, :].rearrange("(p j) c -> p j c", j=4))
-        load_words(1)
-        nc.sync.dma_start(out=w1_raw0[:], in_=w1[0:512, :].rearrange("(p j) c -> p j c", j=4))
-        for u in range(2):
-            nc.sync.dma_start(
-                out=w1_raw1[u][:], in_=w1[512:1024, :].rearrange("(p j) c -> p j c", j=4)[:, :, 256 * u : 256 * (u + 1)]
-            )
+        load_table_words(0)
+        load_scale_rows(nc.scalar, tab_sc, tab_scales)
+        nc.sync.dma_start(out=w3_raw[0][:], in_=weight_pass(w3, 0))
+        load_scale_rows(nc.sync, w2s, w2_scales)
         nc.sync.dma_start(
-            out=w2c[:].bitcast(I32).rearrange("p (a c) -> p a c", a=2), in_=w2_words.bitcast(I32).rearrange("a p c -> p a c")
+            out=w2c[:].bitcast(I32).rearrange("p (a c) -> p a c", a=PASSES), in_=w2_words.bitcast(I32).rearrange("a p c -> p a c")
         )
+        nc.sync.dma_start(out=w3_raw[1][:], in_=weight_pass(w3, 1))
+        load_table_words(1)
+        nc.sync.dma_start(out=w1_raw0[:], in_=weight_pass(w1, 0))
+        for u in range(2):
+            nc.sync.dma_start(out=w1_raw1[u][:], in_=weight_pass(w1, 1)[:, :, H // 2 * u : H // 2 * (u + 1)])
         nc.sync.dma_start(out=w4c[:], in_=w4_words[0].rearrange("p c i -> p (c i)").bitcast(I32))
-        for q in range(4):
+        for q in range(QUADRANTS):
             nc.sync.dma_start(out=w4s[32 * q : 32 * q + 4, :].bitcast(I32), in_=w4_scales.bitcast(I32)[0, 4 * q : 4 * q + 4, :])
 
-        def gather_words(a, j0, n):
-            if (a, j0) == (1, 512):
-                v[a, j0] = shared.tile([P, n], U32, name="v_late", align_bytes=64, offset=0)
+        v, v_sc = {}, {}
+
+        def gather_words(a, j0):
+            if (a, j0) == (1, HALF):
+                v[a, j0] = shared.tile([P, HALF], U32, name="v_late", align_bytes=64, offset=0)
             else:
-                v[a, j0] = keep.tile([P, n], U32, name="v%d_%d" % (a, j0), align_bytes=64)
-            nc.vector.tensor_copy(v[a, j0][:], tab[a][:].bitcast(U32).indirect(list1[:, j0 // 16 : (j0 + n) // 16]))
+                v[a, j0] = keep.tile([P, HALF], U32, name="v%d_%d" % (a, j0), align_bytes=64)
+            nc.vector.tensor_copy(v[a, j0][:], tab[a][:].bitcast(U32).indirect(list_slice(list1, j0, HALF)))
 
-        def walk_out(dst):
-            return dst.rearrange("p (c i) t -> p c t i", i=4)
-
-        def walk_in(src):
-            return src.rearrange("p t (c i) -> p c t i", i=4)
-
-        def quantize(key):
-            grouped, codes, scales = wq[key]
-            nc.vector.quantize_mx(out=codes[:].bitcast(FP8X4), scales=scales[:], in_=grouped[:].rearrange("p c t -> p (c t)"))
-
-        def gather_scales(a, j0, n):
-            if j0 == 512:
-                v_sc[a, j0] = shared.tile([P, n], U8, name="v_sc_late%d" % a, align_bytes=64, offset=2048 + 512 * a)
+        def gather_scales(a, j0):
+            if j0 == HALF:
+                v_sc[a, j0] = shared.tile([P, HALF], U8, name="v_sc_late%d" % a, align_bytes=64, offset=4 * HALF + HALF * a)
             else:
-                v_sc[a, j0] = keep.tile([P, n], U8, name="v_sc%d_%d" % (a, j0), align_bytes=64)
-            nc.vector.tensor_copy(
-                v_sc[a, j0][:], tab_sc[:, T * a : T * (a + 1)].indirect(list1[:, j0 // 16 : (j0 + n) // 16])
-            )
+                v_sc[a, j0] = keep.tile([P, HALF], U8, name="v_sc%d_%d" % (a, j0), align_bytes=64)
+            nc.vector.tensor_copy(v_sc[a, j0][:], tab_sc[:, T * a : T * (a + 1)].indirect(list_slice(list1, j0, HALF)))
 
-        for a in range(2):
-            gather_scales(a, 0, 512)
-        for a in range(2):
-            gather_words(a, 0, 512)
-        for a in range(2):
-            nc.scalar.copy(walk_out(wq["w3", a][0][:]), walk_in(w3_raw[a][:]))
-            quantize(("w3", a))
-        nc.vector.tensor_copy(walk_out(wq["w1", 0][0][:]), walk_in(w1_raw0[:]))
-        quantize(("w1", 0))
+        def quantize(words, scale_bytes, values):
+            nc.vector.quantize_mx(out=words.bitcast(FP8X4), scales=scale_bytes, in_=values.rearrange("p c t -> p (c t)"))
+
+        for a in range(PASSES):
+            gather_scales(a, 0)
+        for a in range(PASSES):
+            gather_words(a, 0)
+        for a in range(PASSES):
+            nc.scalar.copy(walk_out(rounded["w3", a][:]), walk_in(w3_raw[a][:]))
+            quantize(codes["w3", a][:], scales["w3", a][:], rounded["w3", a][:])
+        nc.vector.tensor_copy(walk_out(rounded["w1", 0][:]), walk_in(w1_raw0[:]))
+        quantize(codes["w1", 0][:], scales["w1", 0][:], rounded["w1", 0][:])
         for u in range(2):
             if u == 0:
-                grouped = keep.tile([P, H // 2, 4], BF16, name="w1_first", align_bytes=64)
+                half = keep.tile([P, H // 2, PACK], BF16, name="w1_first", align_bytes=64)
+                pieces = ((0, H // 2),)
             else:
-                grouped = shared.tile([P, H // 2, 4], BF16, name="w1_last", align_bytes=64, offset=1024)
-            nc.vector.tensor_copy(walk_out(grouped[:]), walk_in(w1_raw1[u][:]))
-            cols = slice(256 * u, 256 * (u + 1))
-            nc.vector.quantize_mx(
-                out=wq["w1", 1][1][:, cols].bitcast(FP8X4), scales=wq["w1", 1][2][:, cols], in_=grouped[:].rearrange("p c t -> p (c t)")
-            )
+                half = shared.tile([P, H // 2, PACK], BF16, name="w1_last", align_bytes=64, offset=2 * HALF)
+                pieces = ((0, H // 4), (H // 4, H // 2))
+            for c0, c1 in pieces:
+                nc.vector.tensor_copy(walk_out(half[:, c0:c1, :]), walk_in(w1_raw1[u][:, :, c0:c1]))
+            for c0, c1 in pieces:
+                cols = slice(H // 2 * u + c0, H // 2 * u + c1)
+                quantize(codes["w1", 1][:, cols], scales["w1", 1][:, cols], half[:, c0:c1, :])
+
         wgs_sb = keep.tile([P, S], F32, name="wgs_sb", tag="w3_raw0")
         wgt_sb = keep.tile([P, PM], F32, name="wgt_sb", tag="w1_raw10")
-        surf_sb = [keep.tile([P, 4, PM // 2], F32, name="surf_sb", tag=tag) for tag in ("w3_raw1", "w1_raw0")]
+        surf_sb = [keep.tile([P, PACK, PM // 2], F32, name="surf_sb", tag=tag) for tag in ("w3_raw1", "w1_raw0")]
         nc.sync.dma_start(out=wgs_sb[:], in_=wgs)
         nc.sync.dma_start(out=wgt_sb[:], in_=wgt)
         for u in range(2):
-            nc.sync.dma_start(out=surf_sb[u][:], in_=surf.rearrange("(p t) m -> p t m", t=4)[:, :, 512 * u : 512 * (u + 1)])
-        for t in range(4):
+            nc.sync.dma_start(
+                out=surf_sb[u][:], in_=surf.rearrange("(p t) m -> p t m", t=PACK)[:, :, PM // 2 * u : PM // 2 * (u + 1)]
+            )
+        for t in range(PACK):
             nc.vector.memset(pages[t][:], 0.0)
-        for a in range(2):
-            gather_words(a, 512, 512)
-            gather_scales(a, 512, 512)
+        for a in range(PASSES):
+            gather_words(a, HALF)
+            gather_scales(a, HALF)
 
         def bank_tag(role, j0):
             i = j0 // P
             return "bank%d" % (4 * (i % 2) + (role + 2 * min(i // 2, 1)) % 4)
 
-        def product(tag, j0, fp4):
-            bank = psum.tile([P, H], F32, name=tag, tag=bank_tag({"w2": 0, "w3": 1, "w1": 2}[tag], j0))
-            for a in range(2):
-                if fp4:
+        def product(role, j0):
+            bank = psum.tile([P, H], F32, name="product", tag=bank_tag(role, j0))
+            first = j0 // HALF * HALF
+            cols = slice(j0 - first, j0 - first + P)
+            for a in range(PASSES):
+                if role == MORE:
                     rhs = w2c[:, 2 * H * a : 2 * H * (a + 1)].bitcast(FP4X4)
-                    rhs_sc = w2s[:, H * a : H * (a + 1)]
+                    rhs_scale = w2s[:, H * a : H * (a + 1)]
                 else:
-                    rhs = wq[tag, a][1][:].bitcast(FP8X4)
-                    rhs_sc = wq[tag, a][2][:]
+                    name = "w1" if role == BASE else "w3"
+                    rhs = codes[name, a][:].bitcast(FP8X4)
+                    rhs_scale = scales[name, a][:]
                 nc.tensor.matmul_mx(
-                    out=bank[:], lhsT=v[a, j0 // 512 * 512][:, j0 % 512 : j0 % 512 + P].bitcast(FP8X4), lhsT_scale=v_sc[a, j0 // 512 * 512][:, j0 % 512 : j0 % 512 + P],
-                    rhs=rhs, rhs_scale=rhs_sc, start=(a == 0), stop=(a == 1),
+                    out=bank[:],
+                    lhsT=v[a, first][:, cols].bitcast(FP8X4),
+                    lhsT_scale=v_sc[a, first][:, cols],
+                    rhs=rhs,
+                    rhs_scale=rhs_scale,
+                    start=(a == 0),
+                    stop=(a == PASSES - 1),
                 )
-            return bank[:].rearrange("j (m t) -> j t m", t=4)
+            return bank[:].rearrange("j (p t) -> j t p", t=PACK)
 
-        def token_tile(j0, h_out):
-            more = ring.tile([P, 4, P], F32, name="more", tag="more", bufs=2)
-            less = ring.tile([P, 4, P], F32, name="less", tag="less", bufs=2)
-            neg = ring.tile([P, 4, P], F32, name="neg", tag="neg", bufs=2)
-            base = ring.tile([P, 4, P], F32, name="base", tag="base", bufs=2)
-            nc.scalar.activation(more[:], product("w2", j0, True), ACT.Abs)
-            nc.scalar.activation(less[:], product("w3", j0, False), ACT.Abs)
+        def token_tile(j0, h):
+            more = ring.tile([P, PACK, P], F32, name="more", tag="more", bufs=3)
+            less = ring.tile([P, PACK, P], F32, name="less", tag="less", bufs=2)
+            neg = ring.tile([P, PACK, P], F32, name="neg", tag="neg", bufs=3)
+            base = ring.tile([P, PACK, P], F32, name="base", tag="base", bufs=3)
+            nc.scalar.activation(more[:], product(MORE, j0), ACT.Abs)
+            nc.scalar.activation(less[:], product(LESS, j0), ACT.Abs)
             nc.scalar.activation(neg[:], less[:], ACT.Copy, scale=-1.0)
-            nc.scalar.copy(base[:], product("w1", j0, False))
-            acc = psum.tile([P, 4, P], F32, name="acc", tag=bank_tag(3, j0))
-            for e, term in enumerate((neg, more, base) if j0 == 0 else (base, more, neg)):
-                for t in range(4):
+            base_bank = product(BASE, j0)
+            parts = ((0, 2), (2, PACK)) if j0 == 0 else ((0, PACK),)
+            terms = (neg, more, base) if j0 == 0 else (base, more, neg)
+            for t0, t1 in parts:
+                nc.scalar.copy(base[:, t0:t1, :], base_bank[:, t0:t1, :])
+            total = psum.tile([P, PACK, P], F32, name="total", tag=bank_tag(SUM, j0))
+            for e, term in enumerate(terms):
+                for t in range(PACK):
                     nc.tensor.matmul(
-                        acc[:, t, :], term[:, t, :], ident[:], is_transpose=True, start=(e == 0 and t == 0), stop=(e == 2 and t == 3)
+                        total[:, t, :],
+                        term[:, t, :],
+                        ident[:],
+                        is_transpose=True,
+                        start=(e == 0 and t == 0),
+                        stop=(e == len(terms) - 1 and t == PACK - 1),
                     )
-            nc.scalar.copy(h_out, acc[:])
+            for t0, t1 in parts:
+                nc.scalar.copy(h[:, t0:t1, :], total[:, t0:t1, :])
 
-        j0 = 0
-        for ci, n in enumerate(SCATTER_CHUNKS):
-            h = keep.tile([P, 4, n], F32, name="h%d" % ci)
-            for u in range(n // P):
-                token_tile(j0 + P * u, h[:, :, P * u : P * (u + 1)])
-            for t in range(4):
-                nc.vector.tensor_tensor(
-                    pages[t][:].indirect(list2[:, j0 // 16 : (j0 + n) // 16]), h[:, t, :], wgs_sb[:, j0 : j0 + n], ALU.mult
-                )
-            j0 += n
+        for j0 in range(0, S, P):
+            h = keep.tile([P, PACK, P], F32, name="h%d" % (j0 // P))
+            token_tile(j0, h)
+            for t in range(PACK):
+                nc.vector.tensor_tensor(pages[t][:].indirect(list_slice(list2, j0, P)), h[:, t, :], wgs_sb[:, j0 : j0 + P], ALU.mult)
 
-        starts = [sum(GATHER_CHUNKS[:c]) for c in range(len(GATHER_CHUNKS))]
-        last = len(GATHER_CHUNKS) - 1
+        starts = [sum(CHUNKS[:c]) for c in range(len(CHUNKS))]
+        last = len(CHUNKS) - 1
         xs, zs, zq = {}, {}, {}
 
-        def gather(c):
-            m0, n = starts[c], GATHER_CHUNKS[c]
-            x = ring.tile([P, 4, n], F32, name="x", tag="x", bufs=2)
-            for t in range(4):
+        def gather_x(c):
+            m0, n = starts[c], CHUNKS[c]
+            xs[c] = keep.tile([P, PACK, n], F32, name="x", tag="x")
+            for t in range(PACK):
                 nc.vector.tensor_tensor(
-                    x[:, t, :], pages[t][:].indirect(list3[:, m0 // 16 : (m0 + n) // 16]), wgt_sb[:, m0 : m0 + n], ALU.mult
+                    xs[c][:, t, :], pages[t][:].indirect(list_slice(list3, m0, n)), wgt_sb[:, m0 : m0 + n], ALU.mult
                 )
-            xs[c] = x
 
         def maximum(c):
-            m0, n = starts[c], GATHER_CHUNKS[c]
-            s = surf_sb[m0 // 512][:, :, m0 % 512 : m0 % 512 + n]
-            z = keep.tile([P, n, 4], BF16, name="z%d" % c, align_bytes=64)
+            m0, n = starts[c], CHUNKS[c]
+            within = m0 % (PM // 2)
+            surface = surf_sb[m0 // (PM // 2)][:, :, within : within + n]
+            zs[c] = keep.tile([P, n, PACK], BF16, name="z%d" % c, align_bytes=64)
             if c == last:
-                nc.vector.tensor_tensor(walk_out(z[:]), walk_in(xs[c][:]), walk_in(s), ALU.max)
+                nc.vector.tensor_tensor(walk_out(zs[c][:]), walk_in(xs[c][:]), walk_in(surface), ALU.max)
             else:
-                planes = keep.tile([P, 4, n], BF16, name="planes", tag="planes", align_bytes=64)
-                nc.vector.tensor_tensor(planes[:], xs[c][:], s, ALU.max)
-                nc.scalar.copy(walk_out(z[:]), walk_in(planes[:]))
-            zs[c] = z
+                planes = keep.tile([P, PACK, n], BF16, name="planes", tag="planes", align_bytes=64)
+                nc.vector.tensor_tensor(planes[:], xs[c][:], surface, ALU.max)
+                nc.scalar.copy(walk_out(zs[c][:]), walk_in(planes[:]))
 
         def quantize_z(c):
-            n = GATHER_CHUNKS[c]
-            zc = keep.tile([P, n], U32, name="zc%d" % c, align_bytes=64)
-            zsc = keep.tile([P, n], U8, name="zsc%d" % c, align_bytes=64)
-            nc.vector.quantize_mx(out=zc[:].bitcast(FP8X4), scales=zsc[:], in_=zs[c][:].rearrange("p m t -> p (m t)"))
-            zq[c] = (zc, zsc)
+            n = CHUNKS[c]
+            z_codes = keep.tile([P, n], U32, name="zc%d" % c, align_bytes=64)
+            z_scales = keep.tile([P, n], U8, name="zsc%d" % c, align_bytes=64)
+            quantize(z_codes[:], z_scales[:], zs[c][:])
+            zq[c] = (z_codes, z_scales)
 
         def finish(c):
-            m0, n = starts[c], GATHER_CHUNKS[c]
-            zc, zsc = zq[c]
-            res = keep.tile([P, 3, n], F32, name="res%d" % c)
-            per_bank = min(3, 512 // n)
-            for b0 in range(0, 3, per_bank):
-                nb = min(per_bank, 3 - b0)
-                bank = psum.tile([P, nb, n], F32, name="y", tag="bank%d" % ((2 * c + b0 // per_bank) % 8))
-                for b in range(nb):
+            m0, n = starts[c], CHUNKS[c]
+            z_codes, z_scales = zq[c]
+            res = keep.tile([P, BLOCKS, n], F32, name="res%d" % c)
+            per_bank = min(BLOCKS, BANK // n)
+            for b0 in range(0, BLOCKS, per_bank):
+                count = min(per_bank, BLOCKS - b0)
+                y = psum.tile([P, count, n], F32, name="y", tag="bank%d" % ((2 * c + b0 // per_bank) % 8))
+                for b in range(count):
                     cols = slice(P * (b0 + b), P * (b0 + b + 1))
                     nc.tensor.matmul_mx(
-                        out=bank[:, b, :], lhsT=w4c[:, cols].bitcast(FP8X4), lhsT_scale=w4s[:, cols],
-                        rhs=zc[:].bitcast(FP8X4), rhs_scale=zsc[:], start=True, stop=True,
+                        out=y[:, b, :],
+                        lhsT=w4c[:, cols].bitcast(FP8X4),
+                        lhsT_scale=w4s[:, cols],
+                        rhs=z_codes[:].bitcast(FP8X4),
+                        rhs_scale=z_scales[:],
+                        start=True,
+                        stop=True,
                     )
-                nc.scalar.activation(res[:, b0 : b0 + nb, :], bank[:], ACT.Tanh)
-            nc.sync.dma_start(out=out.rearrange("(b p) m -> p b m", p=P)[:, :, m0 : m0 + n], in_=res[:])
+                nc.scalar.activation(res[:, b0 : b0 + count, :], y[:], ACT.Tanh)
+            queue = nc.scalar if c == last else nc.sync
+            queue.dma_start(out=out.rearrange("(b p) m -> p b m", p=P)[:, :, m0 : m0 + n], in_=res[:])
 
         for c in range(last + 1):
-            gather(c)
+            gather_x(c)
             if c >= 1:
                 quantize_z(c - 1)
             maximum(c)

from contextlib import ExitStack

import concourse.mybir as mybir
from concourse.masks import make_identity

T, S, T2, PM, H, N = 2048, 1024, 2048, 1024, 512, 384
FLOPS = 3623878656

F32 = mybir.dt.float32
BF16 = mybir.dt.bfloat16
I32 = mybir.dt.int32
U32 = mybir.dt.uint32
U16 = mybir.dt.uint16
U8 = mybir.dt.uint8
FP8X4 = mybir.dt.float8_e4m3fn_x4
FP4X4 = mybir.dt.float4_e2m1fn_x4
ACT = mybir.ActivationFunctionType
ALU = mybir.AluOpType

P = 128
PACK = 4
PASSES = 2
K_PASS = P * PACK
QUADRANTS = 4
HALF = S // 2
BANK = 512
BLOCKS = N // P
CHUNKS = (256, 256, 256, 128, 128)
MORE, LESS, BASE, SUM = 0, 1, 2, 3


def list_slice(offsets, first, count):
    return offsets[:, first // 16 : (first + count) // 16]


def walk_out(dst):
    return dst.rearrange("p (c i) t -> p c t i", i=4)


def walk_in(src):
    return src.rearrange("p t (c i) -> p c t i", i=4)


def tile_list_obstacle_fault_scores_kernel(
    tc, tab_words, tab_scales, offs, w1, w2_words, w2_scales, w3, wgs, offs2, wgt, offs3, surf, w4_words, w4_scales, out
):
    nc = tc.nc
    with ExitStack() as ctx:
        keep = ctx.enter_context(tc.tile_pool(name="keep", bufs=1))
        ring = ctx.enter_context(tc.tile_pool(name="ring", bufs=2))
        shared = ctx.enter_context(tc.tile_pool(name="shared", bufs=1))
        psum = ctx.enter_context(tc.psum_pool(name="psum", bufs=1))

        list1 = keep.tile([P, S // 16], U16, name="list1")
        list2 = keep.tile([P, S // 16], U16, name="list2")
        list3 = keep.tile([P, PM // 16], U16, name="list3")
        tab = [keep.tile([P, T], I32, name="tab%d" % a, align_bytes=64) for a in range(PASSES)]
        tab_sc = keep.tile([P, PASSES * T], U8, name="tab_sc", align_bytes=64)
        w2c = keep.tile([P, PASSES * 2 * H], U8, name="w2c", align_bytes=64)
        w2s = keep.tile([P, PASSES * H], U8, name="w2s", align_bytes=64)
        w4c = keep.tile([P, N], I32, name="w4c", align_bytes=64)
        w4s = keep.tile([P, N], U8, name="w4s", align_bytes=64)
        w3_raw = [keep.tile([P, PACK, H], F32, name="w3_raw%d" % a) for a in range(PASSES)]
        w1_raw0 = keep.tile([P, PACK, H], F32, name="w1_raw0")
        w1_raw1 = [keep.tile([P, PACK, H // 2], F32, name="w1_raw1%d" % u) for u in range(2)]
        rounded, codes, scales = {}, {}, {}
        for name in ("w1", "w3"):
            for a in range(PASSES):
                if (name, a) != ("w1", 1):
                    rounded[name, a] = keep.tile([P, H, PACK], BF16, name="%sb%d" % (name, a), align_bytes=64)
                codes[name, a] = keep.tile([P, H], U32, name="%sc%d" % (name, a), align_bytes=64)
                scales[name, a] = keep.tile([P, H], U8, name="%ss%d" % (name, a), align_bytes=64)
        pages = [keep.tile([P, T2], F32, name="page%d" % t) for t in range(PACK)]
        ident = keep.tile([P, P], F32, name="ident")

        nc.gpsimd.memset(tab_sc[:, 0:T].bitcast(I32), 0)
        nc.vector.memset(tab_sc[:, T : 2 * T].bitcast(I32), 0)
        nc.gpsimd.memset(w2s[:].bitcast(I32), 0)
        nc.gpsimd.memset(w4s[:].bitcast(I32), 0)
        make_identity(nc, ident[:])

        def load_table_words(a):
            nc.sync.dma_start(out=tab[a][:], in_=tab_words[a].rearrange("p t i -> p (t i)").bitcast(I32))

        def load_scale_rows(queue, tile, rows):
            for q in range(QUADRANTS):
                queue.dma_start(
                    out=tile[32 * q : 32 * q + 4, :].bitcast(I32).rearrange("r (a c) -> r a c", a=PASSES),
                    in_=rows.bitcast(I32)[:, 4 * q : 4 * q + 4, :].rearrange("a r c -> r a c"),
                )

        def weight_pass(w, a):
            return w[K_PASS * a : K_PASS * (a + 1), :].rearrange("(p i) c -> p i c", i=PACK)

        nc.sync.dma_start(list1[:], offs)
        nc.sync.dma_start(list2[:], offs2)
        nc.sync.dma_start(list3[:], offs3)
        load_table_words(0)
        load_scale_rows(nc.scalar, tab_sc, tab_scales)
        nc.sync.dma_start(out=w3_raw[0][:], in_=weight_pass(w3, 0))
        load_scale_rows(nc.sync, w2s, w2_scales)
        nc.sync.dma_start(
            out=w2c[:].bitcast(I32).rearrange("p (a c) -> p a c", a=PASSES), in_=w2_words.bitcast(I32).rearrange("a p c -> p a c")
        )
        nc.sync.dma_start(out=w3_raw[1][:], in_=weight_pass(w3, 1))
        load_table_words(1)
        nc.sync.dma_start(out=w1_raw0[:], in_=weight_pass(w1, 0))
        for u in range(2):
            nc.sync.dma_start(out=w1_raw1[u][:], in_=weight_pass(w1, 1)[:, :, H // 2 * u : H // 2 * (u + 1)])
        nc.sync.dma_start(out=w4c[:], in_=w4_words[0].rearrange("p c i -> p (c i)").bitcast(I32))
        for q in range(QUADRANTS):
            nc.sync.dma_start(out=w4s[32 * q : 32 * q + 4, :].bitcast(I32), in_=w4_scales.bitcast(I32)[0, 4 * q : 4 * q + 4, :])

        v, v_sc = {}, {}

        def gather_words(a, j0):
            if (a, j0) == (1, HALF):
                v[a, j0] = shared.tile([P, HALF], U32, name="v_late", align_bytes=64, offset=0)
            else:
                v[a, j0] = keep.tile([P, HALF], U32, name="v%d_%d" % (a, j0), align_bytes=64)
            nc.vector.tensor_copy(v[a, j0][:], tab[a][:].bitcast(U32).indirect(list_slice(list1, j0, HALF)))

        def gather_scales(a, j0):
            if j0 == HALF:
                v_sc[a, j0] = shared.tile([P, HALF], U8, name="v_sc_late%d" % a, align_bytes=64, offset=4 * HALF + HALF * a)
            else:
                v_sc[a, j0] = keep.tile([P, HALF], U8, name="v_sc%d_%d" % (a, j0), align_bytes=64)
            nc.vector.tensor_copy(v_sc[a, j0][:], tab_sc[:, T * a : T * (a + 1)].indirect(list_slice(list1, j0, HALF)))

        def quantize(words, scale_bytes, values):
            nc.vector.quantize_mx(out=words.bitcast(FP8X4), scales=scale_bytes, in_=values.rearrange("p c t -> p (c t)"))

        for a in range(PASSES):
            gather_scales(a, 0)
        for a in range(PASSES):
            gather_words(a, 0)
        for a in range(PASSES):
            nc.scalar.copy(walk_out(rounded["w3", a][:]), walk_in(w3_raw[a][:]))
            quantize(codes["w3", a][:], scales["w3", a][:], rounded["w3", a][:])
        nc.vector.tensor_copy(walk_out(rounded["w1", 0][:]), walk_in(w1_raw0[:]))
        quantize(codes["w1", 0][:], scales["w1", 0][:], rounded["w1", 0][:])
        for u in range(2):
            if u == 0:
                half = keep.tile([P, H // 2, PACK], BF16, name="w1_first", align_bytes=64)
                pieces = ((0, H // 2),)
            else:
                half = shared.tile([P, H // 2, PACK], BF16, name="w1_last", align_bytes=64, offset=2 * HALF)
                pieces = ((0, H // 4), (H // 4, H // 2))
            for c0, c1 in pieces:
                nc.vector.tensor_copy(walk_out(half[:, c0:c1, :]), walk_in(w1_raw1[u][:, :, c0:c1]))
            for c0, c1 in pieces:
                cols = slice(H // 2 * u + c0, H // 2 * u + c1)
                quantize(codes["w1", 1][:, cols], scales["w1", 1][:, cols], half[:, c0:c1, :])

        wgs_sb = keep.tile([P, S], F32, name="wgs_sb", tag="w3_raw0")
        wgt_sb = keep.tile([P, PM], F32, name="wgt_sb", tag="w1_raw10")
        surf_sb = [keep.tile([P, PACK, PM // 2], F32, name="surf_sb", tag=tag) for tag in ("w3_raw1", "w1_raw0")]
        nc.sync.dma_start(out=wgs_sb[:], in_=wgs)
        nc.sync.dma_start(out=wgt_sb[:], in_=wgt)
        for u in range(2):
            nc.sync.dma_start(
                out=surf_sb[u][:], in_=surf.rearrange("(p t) m -> p t m", t=PACK)[:, :, PM // 2 * u : PM // 2 * (u + 1)]
            )
        for t in range(PACK):
            nc.vector.memset(pages[t][:], 0.0)
        for a in range(PASSES):
            gather_words(a, HALF)
            gather_scales(a, HALF)

        def bank_tag(role, j0):
            i = j0 // P
            return "bank%d" % (4 * (i % 2) + (role + 2 * min(i // 2, 1)) % 4)

        def product(role, j0):
            bank = psum.tile([P, H], F32, name="product", tag=bank_tag(role, j0))
            first = j0 // HALF * HALF
            cols = slice(j0 - first, j0 - first + P)
            for a in range(PASSES):
                if role == MORE:
                    rhs = w2c[:, 2 * H * a : 2 * H * (a + 1)].bitcast(FP4X4)
                    rhs_scale = w2s[:, H * a : H * (a + 1)]
                else:
                    name = "w1" if role == BASE else "w3"
                    rhs = codes[name, a][:].bitcast(FP8X4)
                    rhs_scale = scales[name, a][:]
                nc.tensor.matmul_mx(
                    out=bank[:],
                    lhsT=v[a, first][:, cols].bitcast(FP8X4),
                    lhsT_scale=v_sc[a, first][:, cols],
                    rhs=rhs,
                    rhs_scale=rhs_scale,
                    start=(a == 0),
                    stop=(a == PASSES - 1),
                )
            return bank[:].rearrange("j (p t) -> j t p", t=PACK)

        def token_tile(j0, h):
            more = ring.tile([P, PACK, P], F32, name="more", tag="more", bufs=3)
            less = ring.tile([P, PACK, P], F32, name="less", tag="less", bufs=2)
            neg = ring.tile([P, PACK, P], F32, name="neg", tag="neg", bufs=3)
            base = ring.tile([P, PACK, P], F32, name="base", tag="base", bufs=3)
            nc.scalar.activation(more[:], product(MORE, j0), ACT.Abs)
            nc.scalar.activation(less[:], product(LESS, j0), ACT.Abs)
            nc.scalar.activation(neg[:], less[:], ACT.Copy, scale=-1.0)
            base_bank = product(BASE, j0)
            parts = ((0, 2), (2, PACK)) if j0 == 0 else ((0, PACK),)
            terms = (neg, more, base) if j0 == 0 else (base, more, neg)
            for t0, t1 in parts:
                nc.scalar.copy(base[:, t0:t1, :], base_bank[:, t0:t1, :])
            total = psum.tile([P, PACK, P], F32, name="total", tag=bank_tag(SUM, j0))
            for e, term in enumerate(terms):
                for t in range(PACK):
                    nc.tensor.matmul(
                        total[:, t, :],
                        term[:, t, :],
                        ident[:],
                        is_transpose=True,
                        start=(e == 0 and t == 0),
                        stop=(e == len(terms) - 1 and t == PACK - 1),
                    )
            for t0, t1 in parts:
                nc.scalar.copy(h[:, t0:t1, :], total[:, t0:t1, :])

        for j0 in range(0, S, P):
            h = keep.tile([P, PACK, P], F32, name="h%d" % (j0 // P))
            token_tile(j0, h)
            for t in range(PACK):
                nc.vector.tensor_tensor(pages[t][:].indirect(list_slice(list2, j0, P)), h[:, t, :], wgs_sb[:, j0 : j0 + P], ALU.mult)

        starts = [sum(CHUNKS[:c]) for c in range(len(CHUNKS))]
        last = len(CHUNKS) - 1
        xs, zs, zq = {}, {}, {}

        def gather_x(c):
            m0, n = starts[c], CHUNKS[c]
            xs[c] = keep.tile([P, PACK, n], F32, name="x", tag="x")
            for t in range(PACK):
                nc.vector.tensor_tensor(
                    xs[c][:, t, :], pages[t][:].indirect(list_slice(list3, m0, n)), wgt_sb[:, m0 : m0 + n], ALU.mult
                )

        def maximum(c):
            m0, n = starts[c], CHUNKS[c]
            within = m0 % (PM // 2)
            surface = surf_sb[m0 // (PM // 2)][:, :, within : within + n]
            zs[c] = keep.tile([P, n, PACK], BF16, name="z%d" % c, align_bytes=64)
            if c == last:
                nc.vector.tensor_tensor(walk_out(zs[c][:]), walk_in(xs[c][:]), walk_in(surface), ALU.max)
            else:
                planes = keep.tile([P, PACK, n], BF16, name="planes", tag="planes", align_bytes=64)
                nc.vector.tensor_tensor(planes[:], xs[c][:], surface, ALU.max)
                nc.scalar.copy(walk_out(zs[c][:]), walk_in(planes[:]))

        def quantize_z(c):
            n = CHUNKS[c]
            z_codes = keep.tile([P, n], U32, name="zc%d" % c, align_bytes=64)
            z_scales = keep.tile([P, n], U8, name="zsc%d" % c, align_bytes=64)
            quantize(z_codes[:], z_scales[:], zs[c][:])
            zq[c] = (z_codes, z_scales)

        def finish(c):
            m0, n = starts[c], CHUNKS[c]
            z_codes, z_scales = zq[c]
            res = keep.tile([P, BLOCKS, n], F32, name="res%d" % c)
            per_bank = min(BLOCKS, BANK // n)
            for b0 in range(0, BLOCKS, per_bank):
                count = min(per_bank, BLOCKS - b0)
                y = psum.tile([P, count, n], F32, name="y", tag="bank%d" % ((2 * c + b0 // per_bank) % 8))
                for b in range(count):
                    cols = slice(P * (b0 + b), P * (b0 + b + 1))
                    nc.tensor.matmul_mx(
                        out=y[:, b, :],
                        lhsT=w4c[:, cols].bitcast(FP8X4),
                        lhsT_scale=w4s[:, cols],
                        rhs=z_codes[:].bitcast(FP8X4),
                        rhs_scale=z_scales[:],
                        start=True,
                        stop=True,
                    )
                nc.scalar.activation(res[:, b0 : b0 + count, :], y[:], ACT.Tanh)
            queue = nc.scalar if c == last else nc.sync
            queue.dma_start(out=out.rearrange("(b p) m -> p b m", p=P)[:, :, m0 : m0 + n], in_=res[:])

        for c in range(last + 1):
            gather_x(c)
            if c >= 1:
                quantize_z(c - 1)
            maximum(c)
            if c >= 1:
                finish(c - 1)
        quantize_z(last)
        finish(last)
